import numpy as np
import ml_dtypes


def mxq(x, axis, fmt="e4m3"):
    dtype, down = {"e4m3": (ml_dtypes.float8_e4m3fn, 7), "e5m2": (ml_dtypes.float8_e5m2, 14)}[fmt]
    v = np.moveaxis(np.asarray(x, np.float32).astype(ml_dtypes.bfloat16).astype(np.float64), axis, -1)
    blocks = v.reshape(v.shape[:-1] + (-1, 32))
    amax = np.abs(blocks).max(-1, keepdims=True)
    byte = np.maximum(np.where(amax > 0, np.frexp(amax)[1] - 1 + 127, 0) - down, 1)
    scale = np.exp2(byte - 127.0)
    codes = (blocks / scale).astype(np.float32).astype(dtype).astype(np.float64)
    return np.moveaxis((codes * scale).reshape(v.shape), -1, axis)


WIDE = False


def mx_kscale(k):
    if not WIDE:
        return np.ones(k)
    levels = np.array([10, -10, 5, -5, 0])
    if k % 512:
        return np.exp2(np.random.permutation(np.resize(levels, k // 32))).repeat(32)
    a = np.empty((k // 512, 16))
    for p in range(k // 512):
        a[p, :8] = np.random.permutation(np.resize(levels, 8))
        for g in range(8):
            far = levels[np.abs(levels - a[p, g]) >= 10]
            a[p, g + 8] = far[np.random.randint(len(far))]
    return np.exp2(a.ravel()).repeat(32)


def f64(x):
    return np.asarray(x).astype(np.float64)


def striped(idx):
    return np.tile(idx.reshape(-1, 16).T, (8, 1)).astype(np.uint16)


def unstriped(offs):
    return offs[:16].T.reshape(-1).astype(np.int64)


def pack_weight(w):
    k, n = w.shape
    w = f64(np.asarray(w, np.float32).astype(ml_dtypes.bfloat16)).reshape(k // 32, 32, n)
    amax = np.abs(w).max(1)
    byte = np.clip(np.where(amax > 0, np.frexp(amax)[1] - 1 + 127 - 7, 1), 1, 254)
    scaled = (w * np.exp2(127.0 - byte)[:, None, :]).reshape(k, n).astype(np.float32)
    words = np.ascontiguousarray(scaled.reshape(k // 512, 128, 4, n).transpose(0, 1, 3, 2)).astype(ml_dtypes.float8_e4m3fn).view(np.uint8)
    return words, np.ascontiguousarray(byte.astype(np.uint8).reshape(k // 512, 16, n))


def unpack_weight(words, scales):
    g, p, n, _ = words.shape
    vals = np.ascontiguousarray(words).view(ml_dtypes.float8_e4m3fn).astype(np.float64) * np.repeat(np.exp2(scales.astype(np.float64) - 127.0), 8, axis=1)[..., None]
    return vals.transpose(0, 1, 3, 2).reshape(g * 512, n)


def relu(v):
    return np.maximum(v, 0.0)


K, T, S, V, U = 512, 2048, 512, 256, 256


def setup_inputs():
    n = np.random.standard_normal
    s = mx_kscale(K)[:, None]
    packed_xT = pack_weight(n((K, T)) * s)
    return {
        "x_words": packed_xT[0],
        "x_scales": packed_xT[1],
        "hT": (n((K, V)) / np.sqrt(K) / s).astype(np.float32),
        "gT": (n((K, V)) / np.sqrt(K) / s).astype(np.float32),
        "offs": striped(np.random.permutation(T)[:S]),
        "tree1": striped(np.random.randint(0, S, U)),
        "tree2": striped(np.random.randint(0, S, U)),
        "tree3": striped(np.random.randint(0, S, U)),
    }


def reference(x_words, x_scales, hT, gT, offs, tree1, tree2, tree3):
    hTq = mxq(f64(hT), 0, "e4m3")
    xq = unpack_weight(x_words, x_scales)[:, unstriped(offs)]
    y = hTq.T @ xq
    ee = np.exp(y)
    se = np.log(ee.sum(axis=1, keepdims=True))
    ly = y - se
    gTq = mxq(f64(gT), 0, "e4m3")
    z = gTq.T @ xq
    a = np.exp(z)
    sa = np.log(a.sum(axis=1, keepdims=True))
    lz = z - sa
    dd = ly - lz
    gg = -1.0 * relu(-1.0 * dd)
    return np.exp(gg[:, unstriped(tree1)] + gg[:, unstriped(tree2)] + gg[:, unstriped(tree3)])

@@ -1,0 +1,129 @@
+from contextlib import ExitStack
+
+import concourse.mybir as mybir
+
+K, T, S, V, U = 512, 2048, 512, 256, 256
+FLOPS = 2 * 2 * K * V * S
+
+F32 = mybir.dt.float32
+BF16 = mybir.dt.bfloat16
+I32 = mybir.dt.int32
+U32 = mybir.dt.uint32
+U16 = mybir.dt.uint16
+U8 = mybir.dt.uint8
+FP8X4 = mybir.dt.float8_e4m3fn_x4
+ALU = mybir.AluOpType
+EXP = mybir.ActivationFunctionType.Exp
+
+P = 128
+PACK = 4
+LINE = 4
+BLOCKS = V // P
+
+
+def tile_picked_yacc_prob_p_kernel(
+    tc, x_words, x_scales, hT, gT, offs, tree1, tree2, tree3, out
+):
+    nc = tc.nc
+    with ExitStack() as ctx:
+        keep = ctx.enter_context(tc.tile_pool(name="keep", bufs=1))
+        psum = ctx.enter_context(tc.psum_pool(name="psum", bufs=1))
+
+        def load_list(name, dram):
+            tile = keep.tile(list(dram.shape), U16, name=name)
+            nc.sync.dma_start(tile[:], dram)
+            return tile
+
+        def load_states(name, dram, b):
+            raw = keep.tile([P, PACK, P], F32, name=f"{name}_raw{b}")
+            rows = dram.rearrange("(p j) v -> p j v", j=PACK)
+            nc.sync.dma_start(raw[:], rows[:, :, b * P : (b + 1) * P])
+            return raw
+
+        scale_table = keep.tile([P, T], U8, name="scale_table", align_bytes=64)
+        nc.vector.memset(scale_table[:].bitcast(I32), 0)
+
+        picked = load_list("picked", offs)
+        h_raw = [load_states("h", hT, 0)]
+        for q in range(4):
+            nc.sync.dma_start(
+                scale_table[32 * q : 32 * q + 4, :].bitcast(I32),
+                x_scales[0, 4 * q : 4 * q + 4, :].bitcast(I32),
+            )
+        word_table = keep.tile([P, T], I32, name="word_table", align_bytes=64)
+        nc.sync.dma_start(word_table[:], x_words[0].rearrange("p c r -> p (c r)").bitcast(I32))
+        g_raw = [load_states("g", gT, 0)]
+        h_raw.append(load_states("h", hT, 1))
+        g_raw.append(load_states("g", gT, 1))
+        trees = [load_list(f"tree{i}", t) for i, t in enumerate((tree1, tree2, tree3))]
+
+        def quantise(name, raw):
+            grouped = keep.tile([P, P, PACK], BF16, name=f"{name}_grouped", align_bytes=64)
+            nc.scalar.copy(
+                grouped[:].rearrange("p (c i) j -> p c j i", i=LINE),
+                raw[:].rearrange("p j (c i) -> p c j i", i=LINE),
+            )
+            codes = keep.tile([P, P], U32, name=f"{name}_codes", align_bytes=64)
+            scales = keep.tile([P, P], U8, name=f"{name}_scales", align_bytes=64)
+            nc.vector.quantize_mx(
+                out=codes[:].bitcast(FP8X4),
+                scales=scales[:],
+                in_=grouped[:].rearrange("p c j -> p (c j)"),
+            )
+            return codes, scales
+
+        h_q = [quantise("h0", h_raw[0])]
+        x_scale = keep.tile([P, S], U8, name="x_scale", align_bytes=64)
+        nc.vector.tensor_copy(x_scale[:], scale_table[:].indirect(picked[:]))
+        x_codes = keep.tile([P, S], U32, name="x_codes", align_bytes=64)
+        nc.vector.tensor_copy(x_codes[:], word_table[:].bitcast(U32).indirect(picked[:]))
+
+        g_q = [quantise("g0", g_raw[0])]
+        h_q.append(quantise("h1", h_raw[1]))
+        g_q.append(quantise("g1", g_raw[1]))
+
+        def logits(name, quantised):
+            codes, scales = quantised
+            bank = psum.tile([P, S], F32, name=f"{name}_bank")
+            nc.tensor.matmul_mx(
+                out=bank[:],
+                lhsT=codes[:].bitcast(FP8X4),
+                lhsT_scale=scales[:],
+                rhs=x_codes[:].bitcast(FP8X4),
+                rhs_scale=x_scale[:],
+                start=True,
+                stop=True,
+            )
+            neg = keep.tile([P, S], F32, name=f"{name}_neg")
+            neg_max = keep.tile([P, 1], F32, name=f"{name}_neg_max")
+            nc.vector.tensor_scalar(neg[:], bank[:], -1.0, None, ALU.mult, ALU.min, accum_out=neg_max[:])
+            weights = keep.tile([P, S], BF16, name=f"{name}_weights")
+            total = keep.tile([P, 1], F32, name=f"{name}_total")
+            nc.scalar.activation(weights[:], neg[:], EXP, bias=neg_max[:], scale=-1.0, accum_out=total[:])
+            return bank, neg, neg_max, total
+
+        accept = []
+        for b in range(BLOCKS):
+            y_bank, y_neg, y_neg_max, y_total = logits(f"y{b}", h_q[b])
+            z_bank, z_neg, z_neg_max, z_total = logits(f"z{b}", g_q[b])
+            diff = keep.tile([P, S], F32, name=f"diff{b}")
+            nc.vector.scalar_tensor_tensor(diff[:], z_neg[:], z_neg_max[:], y_bank[:], ALU.subtract, ALU.add)
+            ratio = keep.tile([P, S], F32, name=f"ratio{b}")
+            nc.scalar.activation(ratio[:], diff[:], EXP, bias=y_neg_max[:])
+            inv = keep.tile([P, 1], F32, name=f"inv{b}")
+            nc.vector.reciprocal(inv[:], y_total[:])
+            norm = keep.tile([P, 1], F32, name=f"norm{b}")
+            nc.vector.tensor_tensor(norm[:], inv[:], z_total[:], ALU.mult)
+            accept.append((ratio, norm))
+
+        for b in range(BLOCKS):
+            ratio, norm = accept[b]
+            table = keep.tile([P, S], F32, name=f"accept{b}")
+            nc.vector.tensor_scalar(table[:], ratio[:], norm[:], 1.0, ALU.mult, ALU.min)
+            path = keep.tile([P, U], F32, name=f"path{b}_0")
+            nc.vector.tensor_copy(path[:], table[:].indirect(trees[0][:]))
+            for i in (1, 2):
+                longer = keep.tile([P, U], F32, name=f"path{b}_{i}")
+                nc.vector.tensor_tensor(longer[:], table[:].indirect(trees[i][:]), path[:], ALU.mult)
+                path = longer
+            nc.sync.dma_start(out[b * P : (b + 1) * P, :], path[:])

@@ -14,6 +14,7 @@ U8 = mybir.dt.uint8
 FP8X4 = mybir.dt.float8_e4m3fn_x4
 ALU = mybir.AluOpType
 EXP = mybir.ActivationFunctionType.Exp
+IDENTITY = mybir.ActivationFunctionType.Identity
 
 P = 128
 PACK = 4
@@ -34,37 +35,49 @@ def tile_picked_yacc_prob_p_kernel(
             nc.sync.dma_start(tile[:], dram)
             return tile
 
-        def load_states(name, dram, b):
-            raw = keep.tile([P, PACK, P], F32, name=f"{name}_raw{b}")
-            rows = dram.rearrange("(p j) v -> p j v", j=PACK)
-            nc.sync.dma_start(raw[:], rows[:, :, b * P : (b + 1) * P])
+        def load_states(name, dram):
+            raw = keep.tile([P, PACK, V], F32, name=name, align_bytes=64)
+            nc.sync.dma_start(raw[:], dram.rearrange("(p j) v -> p j v", j=PACK))
             return raw
 
         scale_table = keep.tile([P, T], U8, name="scale_table", align_bytes=64)
-        nc.vector.memset(scale_table[:].bitcast(I32), 0)
+        nc.vector.memset(scale_table[:, : T // 2].bitcast(I32), 0)
+        nc.gpsimd.memset(scale_table[:, T // 2 :].bitcast(I32), 0)
+        warm = keep.tile([P, 1], F32, name="warm")
+        nc.vector.memset(warm[:], 0.0)
+        warmed = keep.tile([P, 1], F32, name="warmed")
+        nc.scalar.activation(warmed[:], warm[:], EXP)
 
         picked = load_list("picked", offs)
-        h_raw = [load_states("h", hT, 0)]
+        word_table = keep.tile([P, T], I32, name="word_table", align_bytes=64)
+        words = x_words[0].rearrange("p c r -> p (c r)").bitcast(I32)
+        for c in (0, T // 2):
+            nc.sync.dma_start(word_table[:, c : c + T // 2], words[:, c : c + T // 2])
         for q in range(4):
             nc.sync.dma_start(
                 scale_table[32 * q : 32 * q + 4, :].bitcast(I32),
                 x_scales[0, 4 * q : 4 * q + 4, :].bitcast(I32),
             )
-        word_table = keep.tile([P, T], I32, name="word_table", align_bytes=64)
-        nc.sync.dma_start(word_table[:], x_words[0].rearrange("p c r -> p (c r)").bitcast(I32))
-        g_raw = [load_states("g", gT, 0)]
-        h_raw.append(load_states("h", hT, 1))
-        g_raw.append(load_states("g", gT, 1))
-        trees = [load_list(f"tree{i}", t) for i, t in enumerate((tree1, tree2, tree3))]
+        trees = [load_list("tree0", tree1)]
+        h_raw = load_states("h_raw", hT)
+        g_raw = load_states("g_raw", gT)
+        trees.append(load_list("tree1", tree2))
+        trees.append(load_list("tree2", tree3))
+
+        x_codes = keep.tile([P, S], U32, name="x_codes", align_bytes=64)
+        nc.vector.tensor_copy(x_codes[:], word_table[:].bitcast(U32).indirect(picked[:]))
+        x_scale = keep.tile([P, S], U8, name="x_scale", align_bytes=64)
+        nc.vector.tensor_copy(x_scale[:], scale_table[:].indirect(picked[:]))
 
         def quantise(name, raw):
-            grouped = keep.tile([P, P, PACK], BF16, name=f"{name}_grouped", align_bytes=64)
+            width = raw.shape[2]
+            grouped = keep.tile([P, width, PACK], BF16, name=f"{name}_grouped", align_bytes=64)
             nc.scalar.copy(
                 grouped[:].rearrange("p (c i) j -> p c j i", i=LINE),
-                raw[:].rearrange("p j (c i) -> p c j i", i=LINE),
+                raw.rearrange("p j (c i) -> p c j i", i=LINE),
             )
-            codes = keep.tile([P, P], U32, name=f"{name}_codes", align_bytes=64)
-            scales = keep.tile([P, P], U8, name=f"{name}_scales", align_bytes=64)
+            codes = keep.tile([P, width], U32, name=f"{name}_codes", align_bytes=64)
+            scales = keep.tile([P, width], U8, name=f"{name}_scales", align_bytes=64)
             nc.vector.quantize_mx(
                 out=codes[:].bitcast(FP8X4),
                 scales=scales[:],
@@ -72,58 +85,71 @@ def tile_picked_yacc_prob_p_kernel(
             )
             return codes, scales
 
-        h_q = [quantise("h0", h_raw[0])]
-        x_scale = keep.tile([P, S], U8, name="x_scale", align_bytes=64)
-        nc.vector.tensor_copy(x_scale[:], scale_table[:].indirect(picked[:]))
-        x_codes = keep.tile([P, S], U32, name="x_codes", align_bytes=64)
-        nc.vector.tensor_copy(x_codes[:], word_table[:].bitcast(U32).indirect(picked[:]))
+        h_q = [quantise(f"h{b}", h_raw[:, :, b * P : (b + 1) * P]) for b in range(BLOCKS)]
+        g_codes, g_scales = quantise("g", g_raw[:])
 
-        g_q = [quantise("g0", g_raw[0])]
-        h_q.append(quantise("h1", h_raw[1]))
-        g_q.append(quantise("g1", g_raw[1]))
-
-        def logits(name, quantised):
-            codes, scales = quantised
+        def logits(name, codes, scales):
             bank = psum.tile([P, S], F32, name=f"{name}_bank")
             nc.tensor.matmul_mx(
                 out=bank[:],
-                lhsT=codes[:].bitcast(FP8X4),
-                lhsT_scale=scales[:],
+                lhsT=codes.bitcast(FP8X4),
+                lhsT_scale=scales,
                 rhs=x_codes[:].bitcast(FP8X4),
                 rhs_scale=x_scale[:],
                 start=True,
                 stop=True,
             )
-            neg = keep.tile([P, S], F32, name=f"{name}_neg")
-            neg_max = keep.tile([P, 1], F32, name=f"{name}_neg_max")
-            nc.vector.tensor_scalar(neg[:], bank[:], -1.0, None, ALU.mult, ALU.min, accum_out=neg_max[:])
-            weights = keep.tile([P, S], BF16, name=f"{name}_weights")
-            total = keep.tile([P, 1], F32, name=f"{name}_total")
-            nc.scalar.activation(weights[:], neg[:], EXP, bias=neg_max[:], scale=-1.0, accum_out=total[:])
-            return bank, neg, neg_max, total
+            return bank
 
-        accept = []
+        def exp_sum(name, source, sign, neg_max, weights_tag):
+            weights = keep.tile([P, S], BF16, name=f"{name}_weights", tag=weights_tag, align_bytes=64)
+            total = keep.tile([P, 1], F32, name=f"{name}_total")
+            nc.scalar.activation(weights[:], source[:], EXP, bias=neg_max[:], scale=sign, accum_out=total[:])
+            return total
+
+        y = []
+        for b, (max_tag, weights_tag) in enumerate((("y0_neg_max", "g_raw"), ("g_grouped", "y1_weights"))):
+            bank = logits(f"y{b}", h_q[b][0][:], h_q[b][1][:])
+            neg_max = keep.tile([P, 1], F32, name=f"y{b}_neg_max", tag=max_tag, align_bytes=64)
+            nc.vector.tensor_reduce(neg_max[:], bank[:], mybir.AxisListType.X, ALU.max, negate=True)
+            y.append((bank, neg_max, exp_sum(f"y{b}", bank, 1.0, neg_max, weights_tag)))
+
+        ratios = []
         for b in range(BLOCKS):
-            y_bank, y_neg, y_neg_max, y_total = logits(f"y{b}", h_q[b])
-            z_bank, z_neg, z_neg_max, z_total = logits(f"z{b}", g_q[b])
-            diff = keep.tile([P, S], F32, name=f"diff{b}")
-            nc.vector.scalar_tensor_tensor(diff[:], z_neg[:], z_neg_max[:], y_bank[:], ALU.subtract, ALU.add)
-            ratio = keep.tile([P, S], F32, name=f"ratio{b}")
-            nc.scalar.activation(ratio[:], diff[:], EXP, bias=y_neg_max[:])
+            y_bank, y_neg_max, y_total = y[b]
+            cols = slice(b * P, (b + 1) * P)
+            z_bank = logits(f"z{b}", g_codes[:, cols], g_scales[:, cols])
+            z_neg = keep.tile([P, S], F32, name=f"z{b}_neg")
+            z_neg_max = keep.tile([P, 1], F32, name=f"z{b}_neg_max")
+            nc.vector.tensor_scalar(z_neg[:], z_bank[:], -1.0, None, ALU.mult, ALU.min, accum_out=z_neg_max[:])
+            z_total = exp_sum(f"z{b}", z_neg, -1.0, z_neg_max, f"z{b}_weights")
             inv = keep.tile([P, 1], F32, name=f"inv{b}")
             nc.vector.reciprocal(inv[:], y_total[:])
+            diff = keep.tile([P, S], F32, name=f"diff{b}")
+            nc.vector.scalar_tensor_tensor(diff[:], z_neg[:], z_neg_max[:], y_bank[:], ALU.subtract, ALU.add)
             norm = keep.tile([P, 1], F32, name=f"norm{b}")
-            nc.vector.tensor_tensor(norm[:], inv[:], z_total[:], ALU.mult)
-            accept.append((ratio, norm))
+            nc.scalar.activation(norm[:], z_total[:], IDENTITY, scale=inv[:])
+            ratio = keep.tile([P, S], F32, name=f"ratio{b}")
+            nc.scalar.activation(ratio[:], diff[:], EXP, bias=y_neg_max[:])
+            ratios.append((ratio, norm))
 
-        for b in range(BLOCKS):
-            ratio, norm = accept[b]
-            table = keep.tile([P, S], F32, name=f"accept{b}")
-            nc.vector.tensor_scalar(table[:], ratio[:], norm[:], 1.0, ALU.mult, ALU.min)
-            path = keep.tile([P, U], F32, name=f"path{b}_0")
-            nc.vector.tensor_copy(path[:], table[:].indirect(trees[0][:]))
-            for i in (1, 2):
-                longer = keep.tile([P, U], F32, name=f"path{b}_{i}")
-                nc.vector.tensor_tensor(longer[:], table[:].indirect(trees[i][:]), path[:], ALU.mult)
-                path = longer
-            nc.sync.dma_start(out[b * P : (b + 1) * P, :], path[:])
+        tables, paths = {}, {}
+
+        def step(b, i):
+            if i == 0:
+                ratio, norm = ratios[b]
+                tables[b] = keep.tile([P, S], F32, name=f"accept{b}")
+                nc.vector.tensor_scalar(tables[b][:], ratio[:], norm[:], 1.0, ALU.mult, ALU.min)
+                return
+            looked_up = tables[b][:].indirect(trees[i - 1][:])
+            longer = keep.tile([P, U], F32, name=f"path{b}_{i}")
+            if i == 1:
+                nc.vector.tensor_copy(longer[:], looked_up)
+            else:
+                nc.vector.tensor_tensor(longer[:], looked_up, paths[b][:], ALU.mult)
+            paths[b] = longer
+            if i == 3:
+                nc.sync.dma_start(out[b * P : (b + 1) * P, :], longer[:])
+
+        for b, i in ((0, 0), (0, 1), (1, 0), (0, 2), (1, 1), (0, 3), (1, 2), (1, 3)):
+            step(b, i)

from contextlib import ExitStack

import concourse.mybir as mybir

K, T, S, V, U = 512, 2048, 512, 256, 256
FLOPS = 2 * 2 * K * V * S

F32 = mybir.dt.float32
BF16 = mybir.dt.bfloat16
I32 = mybir.dt.int32
U32 = mybir.dt.uint32
U16 = mybir.dt.uint16
U8 = mybir.dt.uint8
FP8X4 = mybir.dt.float8_e4m3fn_x4
ALU = mybir.AluOpType
EXP = mybir.ActivationFunctionType.Exp
IDENTITY = mybir.ActivationFunctionType.Identity

P = 128
PACK = 4
LINE = 4
BLOCKS = V // P


def tile_picked_yacc_prob_p_kernel(
    tc, x_words, x_scales, hT, gT, offs, tree1, tree2, tree3, out
):
    nc = tc.nc
    with ExitStack() as ctx:
        keep = ctx.enter_context(tc.tile_pool(name="keep", bufs=1))
        psum = ctx.enter_context(tc.psum_pool(name="psum", bufs=1))

        def load_list(name, dram):
            tile = keep.tile(list(dram.shape), U16, name=name)
            nc.sync.dma_start(tile[:], dram)
            return tile

        def load_states(name, dram):
            raw = keep.tile([P, PACK, V], F32, name=name, align_bytes=64)
            nc.sync.dma_start(raw[:], dram.rearrange("(p j) v -> p j v", j=PACK))
            return raw

        scale_table = keep.tile([P, T], U8, name="scale_table", align_bytes=64)
        nc.vector.memset(scale_table[:, : T // 2].bitcast(I32), 0)
        nc.gpsimd.memset(scale_table[:, T // 2 :].bitcast(I32), 0)
        warm = keep.tile([P, 1], F32, name="warm")
        nc.vector.memset(warm[:], 0.0)
        warmed = keep.tile([P, 1], F32, name="warmed")
        nc.scalar.activation(warmed[:], warm[:], EXP)

        picked = load_list("picked", offs)
        word_table = keep.tile([P, T], I32, name="word_table", align_bytes=64)
        words = x_words[0].rearrange("p c r -> p (c r)").bitcast(I32)
        for c in (0, T // 2):
            nc.sync.dma_start(word_table[:, c : c + T // 2], words[:, c : c + T // 2])
        for q in range(4):
            nc.sync.dma_start(
                scale_table[32 * q : 32 * q + 4, :].bitcast(I32),
                x_scales[0, 4 * q : 4 * q + 4, :].bitcast(I32),
            )
        trees = [load_list("tree0", tree1)]
        h_raw = load_states("h_raw", hT)
        g_raw = load_states("g_raw", gT)
        trees.append(load_list("tree1", tree2))
        trees.append(load_list("tree2", tree3))

        x_codes = keep.tile([P, S], U32, name="x_codes", align_bytes=64)
        nc.vector.tensor_copy(x_codes[:], word_table[:].bitcast(U32).indirect(picked[:]))
        x_scale = keep.tile([P, S], U8, name="x_scale", align_bytes=64)
        nc.vector.tensor_copy(x_scale[:], scale_table[:].indirect(picked[:]))

        def quantise(name, raw):
            width = raw.shape[2]
            grouped = keep.tile([P, width, PACK], BF16, name=f"{name}_grouped", align_bytes=64)
            nc.scalar.copy(
                grouped[:].rearrange("p (c i) j -> p c j i", i=LINE),
                raw.rearrange("p j (c i) -> p c j i", i=LINE),
            )
            codes = keep.tile([P, width], U32, name=f"{name}_codes", align_bytes=64)
            scales = keep.tile([P, width], U8, name=f"{name}_scales", align_bytes=64)
            nc.vector.quantize_mx(
                out=codes[:].bitcast(FP8X4),
                scales=scales[:],
                in_=grouped[:].rearrange("p c j -> p (c j)"),
            )
            return codes, scales

        h_q = [quantise(f"h{b}", h_raw[:, :, b * P : (b + 1) * P]) for b in range(BLOCKS)]
        g_codes, g_scales = quantise("g", g_raw[:])

        def logits(name, codes, scales):
            bank = psum.tile([P, S], F32, name=f"{name}_bank")
            nc.tensor.matmul_mx(
                out=bank[:],
                lhsT=codes.bitcast(FP8X4),
                lhsT_scale=scales,
                rhs=x_codes[:].bitcast(FP8X4),
                rhs_scale=x_scale[:],
                start=True,
                stop=True,
            )
            return bank

        def exp_sum(name, source, sign, neg_max, weights_tag):
            weights = keep.tile([P, S], BF16, name=f"{name}_weights", tag=weights_tag, align_bytes=64)
            total = keep.tile([P, 1], F32, name=f"{name}_total")
            nc.scalar.activation(weights[:], source[:], EXP, bias=neg_max[:], scale=sign, accum_out=total[:])
            return total

        y = []
        for b, (max_tag, weights_tag) in enumerate((("y0_neg_max", "g_raw"), ("g_grouped", "y1_weights"))):
            bank = logits(f"y{b}", h_q[b][0][:], h_q[b][1][:])
            neg_max = keep.tile([P, 1], F32, name=f"y{b}_neg_max", tag=max_tag, align_bytes=64)
            nc.vector.tensor_reduce(neg_max[:], bank[:], mybir.AxisListType.X, ALU.max, negate=True)
            y.append((bank, neg_max, exp_sum(f"y{b}", bank, 1.0, neg_max, weights_tag)))

        ratios = []
        for b in range(BLOCKS):
            y_bank, y_neg_max, y_total = y[b]
            cols = slice(b * P, (b + 1) * P)
            z_bank = logits(f"z{b}", g_codes[:, cols], g_scales[:, cols])
            z_neg = keep.tile([P, S], F32, name=f"z{b}_neg")
            z_neg_max = keep.tile([P, 1], F32, name=f"z{b}_neg_max")
            nc.vector.tensor_scalar(z_neg[:], z_bank[:], -1.0, None, ALU.mult, ALU.min, accum_out=z_neg_max[:])
            z_total = exp_sum(f"z{b}", z_neg, -1.0, z_neg_max, f"z{b}_weights")
            inv = keep.tile([P, 1], F32, name=f"inv{b}")
            nc.vector.reciprocal(inv[:], y_total[:])
            diff = keep.tile([P, S], F32, name=f"diff{b}")
            nc.vector.scalar_tensor_tensor(diff[:], z_neg[:], z_neg_max[:], y_bank[:], ALU.subtract, ALU.add)
            norm = keep.tile([P, 1], F32, name=f"norm{b}")
            nc.scalar.activation(norm[:], z_total[:], IDENTITY, scale=inv[:])
            ratio = keep.tile([P, S], F32, name=f"ratio{b}")
            nc.scalar.activation(ratio[:], diff[:], EXP, bias=y_neg_max[:])
            ratios.append((ratio, norm))

        tables, paths = {}, {}

        def step(b, i):
            if i == 0:
                ratio, norm = ratios[b]
                tables[b] = keep.tile([P, S], F32, name=f"accept{b}")
                nc.vector.tensor_scalar(tables[b][:], ratio[:], norm[:], 1.0, ALU.mult, ALU.min)
                return
            looked_up = tables[b][:].indirect(trees[i - 1][:])
            longer = keep.tile([P, U], F32, name=f"path{b}_{i}")
            if i == 1:
                nc.vector.tensor_copy(longer[:], looked_up)
            else:
                nc.vector.tensor_tensor(longer[:], looked_up, paths[b][:], ALU.mult)
            paths[b] = longer
            if i == 3:
                nc.sync.dma_start(out[b * P : (b + 1) * P, :], longer[:])

        for b, i in ((0, 0), (0, 1), (1, 0), (0, 2), (1, 1), (0, 3), (1, 2), (1, 3)):
            step(b, i)
